import numpy as np, ml_dtypes
CORES = [242,247,114,119]
N = 4
DEG, TK = 2, 256
MASK = [[2,0],[2,1],[2,0],[2,3]]
def setup_inputs(rng):
    return {"x": rng.standard_normal((N, 128, TK), dtype=np.float32).astype(ml_dtypes.bfloat16), "w": rng.standard_normal((N, 128, DEG * 128), dtype=np.float32).astype(ml_dtypes.bfloat16)}
def setup_inputs_big(rng):
    d = setup_inputs(rng)
    for k in ("x", "w"): d[k] = (d[k].astype(np.float32) * 1024.0).astype(d[k].dtype)
    return d
def setup_inputs_small(rng):
    d = setup_inputs(rng)
    for k in ("x", "w"): d[k] = (d[k].astype(np.float32) * (1 / 1024.0)).astype(d[k].dtype)
    return d
def setup_inputs_apart(rng):
    d = setup_inputs(rng)
    f = (10.0 ** rng.permutation(np.linspace(-1.5, 1.5, N))).astype(np.float32).reshape(N, 1, 1)
    for k in ("x", "w"): d[k] = (d[k].astype(np.float32) * f).astype(d[k].dtype)
    return d
def reference(x, w):
    X, W = x.astype(np.float64), w.astype(np.float64)
    y = np.zeros((N, 128, TK))
    for r in range(N):
        for i, j in enumerate(MASK[r]):
            y[r] += W[r][:, 128 * i:128 * i + 128].T @ X[j]
    return {"y": y.astype(ml_dtypes.bfloat16 if x.dtype != np.float64 else np.float64)}

from concourse.bass import DstId, RemoteDMATransfer

P, TK, TILE = 128, 256, 128
SLOTS = 1

SCRATCH = {
    "xd": ("dram", [P, TK], "bfloat16"),
    "xs": ("sbuf", [P, TK], "bfloat16"),
    "ws": ("sbuf", [P, 2 * TILE], "bfloat16"),
    "land": ("sbuf", [P, SLOTS * TK], "bfloat16"),
    "acc": ("psum", [P, TK], "float32"),
    "ys": ("sbuf", [P, TK], "bfloat16"),
}
SEMAPHORES = ["staged", "loaded", "arrived", "sent", "summed", "rounded", "stored"]


def _bits(m):
    return [b for b in range(m.bit_length()) if (m >> b) & 1]


def _pow2_floor(n):
    return 1 << (n.bit_length() - 1)


def _plan(src, dests, topo):
    far = [d for d in dests if (topo.host(d), topo.chip(d)) != (topo.host(src), topo.chip(src))]
    near = [d for d in dests if d not in far]
    plan = {}
    far_eng = []
    if far:
        common = topo.mask(src, far[0])
        for d in far:
            common &= topo.mask(src, d)
        far_eng = _bits(common)
        k = _pow2_floor(len(far_eng) // len(far))
        for n, d in enumerate(far):
            plan[d] = far_eng[n * k:(n + 1) * k]
    if near:
        spare = [b for b in _bits(topo.mask(src, near[0])) if b not in far_eng]
        room = _pow2_floor(len(spare) // len(near))
        k = min(room, len(plan[far[0]])) if far else room
        step = room // k
        for n, d in enumerate(near):
            plan[d] = spare[n * room:(n + 1) * room:step]
    return {d: (sum(1 << b for b in e), len(e)) for d, e in plan.items()}


def rank_program(g, core, T, topo):
    rank = T.rank_of(core)
    if rank is None:
        return
    mask_tab = T.tables["MASK"]
    cores = T.cores
    sem = T.sem

    slot_of = []
    for r, row in enumerate(mask_tab):
        foreign = []
        for j in row:
            if j != r and j not in foreign:
                foreign.append(j)
        assert len(foreign) <= SLOTS
        slot_of.append({j: s for s, j in enumerate(foreign)})
    takers = [r for r in range(len(cores)) if rank in slot_of[r]]

    if takers:
        g.sync.dma_start(T.xd[:], T.x[:]).then_inc(sem.staged, 16)
        g.sync.dma_start(T.xs[:], T.x[:]).then_inc(sem.loaded, 16)
        g.sync.dma_start(T.ws[:], T.w[:]).then_inc(sem.loaded, 16)
    else:
        g.sync.dma_start(T.xs[:], T.x[:]).then_inc(sem.loaded, 16)
        g.scalar.dma_start(T.ws[:], T.w[:]).then_inc(sem.loaded, 16)

    if takers:
        plan = _plan(core, [cores[r] for r in takers], topo)
        transfers = []
        total = 0
        for r in takers:
            d = cores[r]
            rid, pid = topo.addr(d, core)
            m, n = plan[d]
            s = slot_of[r][rank]
            transfers.append(RemoteDMATransfer(dst_ids=[DstId(rid=rid, pnc=pid)], dma_engine_mask=m,
                                               remote_sem=sem.arrived, src=T.xd[:],
                                               dst=T.land[:, s * TK:(s + 1) * TK]))
            total += n
        g.wait_ge(sem.staged, 16)
        g.remote_dma_fused(transfers, local_sem=sem.sent)
        g.wait_ge(sem.sent, total)

    incoming = 0
    for j in slot_of[rank]:
        src = cores[j]
        incoming += _plan(src, [cores[r] for r in range(len(cores)) if j in slot_of[r]], topo)[core][1]

    terms = [(i, j) for i, j in enumerate(mask_tab[rank]) if j == rank]
    n_own = len(terms)
    terms += [(i, j) for i, j in enumerate(mask_tab[rank]) if j != rank]
    g.tensor.wait_ge(sem.loaded, 32)
    for n, (i, j) in enumerate(terms):
        if n == n_own:
            g.tensor.wait_ge(sem.arrived, incoming)
        if j == rank:
            rhs = T.xs[:]
        else:
            s = slot_of[rank][j]
            rhs = T.land[:, s * TK:(s + 1) * TK]
        mm = g.tensor.matmul(T.acc[:], T.ws[:, i * TILE:(i + 1) * TILE], rhs, start=(n == 0), stop=(n == len(terms) - 1))
        if n == len(terms) - 1:
            mm.then_inc(sem.summed, 1)

    g.vector.wait_ge(sem.summed, 1)
    g.vector.tensor_copy(T.ys[:], T.acc[:]).then_inc(sem.rounded, 1)
    g.sync.wait_ge(sem.rounded, 1)
    g.sync.dma_start(T.y[:], T.ys[:]).then_inc(sem.stored, 16)
    g.sync.wait_ge(sem.stored, 16)
